import numpy as np
import ml_dtypes


def mxq(x, axis, fmt="e4m3"):
    dtype, down = {"e4m3": (ml_dtypes.float8_e4m3fn, 7), "e5m2": (ml_dtypes.float8_e5m2, 14)}[fmt]
    v = np.moveaxis(np.asarray(x, np.float32).astype(ml_dtypes.bfloat16).astype(np.float64), axis, -1)
    blocks = v.reshape(v.shape[:-1] + (-1, 32))
    amax = np.abs(blocks).max(-1, keepdims=True)
    byte = np.maximum(np.where(amax > 0, np.frexp(amax)[1] - 1 + 127, 0) - down, 1)
    scale = np.exp2(byte - 127.0)
    codes = (blocks / scale).astype(np.float32).astype(dtype).astype(np.float64)
    return np.moveaxis((codes * scale).reshape(v.shape), -1, axis)


WIDE = False


def mx_kscale(k):
    if not WIDE:
        return np.ones(k)
    levels = np.array([10, -10, 5, -5, 0])
    if k % 512:
        return np.exp2(np.random.permutation(np.resize(levels, k // 32))).repeat(32)
    a = np.empty((k // 512, 16))
    for p in range(k // 512):
        a[p, :8] = np.random.permutation(np.resize(levels, 8))
        for g in range(8):
            far = levels[np.abs(levels - a[p, g]) >= 10]
            a[p, g + 8] = far[np.random.randint(len(far))]
    return np.exp2(a.ravel()).repeat(32)


def f64(x):
    return np.asarray(x).astype(np.float64)


def striped8(idx):
    return np.asarray(idx).reshape(8, -1, 16).transpose(0, 2, 1).reshape(128, -1).astype(np.uint16)


def unstriped8(offs):
    return offs.reshape(8, 16, -1).transpose(0, 2, 1).reshape(8, -1).astype(np.int64)


def pick8(x, idx, run):
    r = np.arange(len(x))
    return x[r[:, None], idx[r % (8 * run) // run]]


E2M1 = np.array([0.0, 0.5, 1.0, 1.5, 2.0, 3.0, 4.0, 6.0, -0.0, -0.5, -1.0, -1.5, -2.0, -3.0, -4.0, -6.0])


def pack_weight(w, fmt):
    k, n = w.shape
    w = f64(np.asarray(w, np.float32).astype(ml_dtypes.bfloat16)).reshape(k // 32, 32, n)
    amax = np.abs(w).max(1)
    if fmt == "e4m3":
        byte = np.frexp(amax)[1] - 1 + 127 - 7
    else:
        mant, ex = np.frexp(amax / 6.0)
        byte = np.where(mant > 0.5, ex, ex - 1) + 127
    byte = np.clip(np.where(amax > 0, byte, 1), 1, 254)
    scaled = (w * np.exp2(127.0 - byte)[:, None, :]).reshape(k, n).astype(np.float32)
    by_word = np.ascontiguousarray(scaled.reshape(k // 512, 128, 4, n).transpose(0, 1, 3, 2))
    if fmt == "e4m3":
        words = by_word.astype(ml_dtypes.float8_e4m3fn).view(np.uint8)
    else:
        c = by_word.astype(ml_dtypes.float4_e2m1fn).view(np.uint8) & 0xF
        words = (c[..., 0::2] | (c[..., 1::2] << 4)).reshape(k // 512, 128, 2 * n)
    return np.ascontiguousarray(words), np.ascontiguousarray(byte.astype(np.uint8).reshape(k // 512, 16, n))


def unpack_weight(words, scales, fmt):
    g, _, n = scales.shape
    words = np.ascontiguousarray(words).reshape(g, 128, n, -1)
    if fmt == "e4m3":
        vals = words.view(ml_dtypes.float8_e4m3fn).astype(np.float64)
    else:
        nib = np.empty((g, 128, n, 4), np.uint8)
        nib[..., 0::2] = words & 0xF
        nib[..., 1::2] = words >> 4
        vals = E2M1[nib]
    vals = vals * np.repeat(np.exp2(scales.astype(np.float64) - 127.0), 8, axis=1)[..., None]
    return vals.transpose(0, 1, 3, 2).reshape(g * 512, n)


def bf(x):
    return np.asarray(x, np.float32).astype(ml_dtypes.bfloat16)


def planes(Y):
    r, m = Y.shape
    b = f64(bf(Y)).reshape(r // 32, 32, m)
    amax = np.abs(b).max(1)
    byte = np.clip(np.where(amax > 0, np.frexp(amax)[1] - 1 + 127 - 7, 1), 1, 254)
    codes = (b * np.exp2(127.0 - byte)[:, None, :]).reshape(r, m).astype(np.float32).astype(ml_dtypes.float8_e4m3fn).view(np.uint8)
    words = codes.reshape(r // 512, 128, 4, m).transpose(0, 1, 3, 2)
    return np.ascontiguousarray(words), np.ascontiguousarray(byte.astype(np.uint8).reshape(r // 512, 16, m))


K, T, J, B, L, N = 512, 2048, 1024, 128, 512, 512


def setup_inputs():
    n = np.random.standard_normal
    idx = np.stack([np.random.permutation(T)[:J] for _ in range(8)])
    fk = mx_kscale(K)
    fl = mx_kscale(L)
    wp = pack_weight(n((K, N)) * 1 / np.sqrt(K) * fk[:, None], "e4m3")
    bxp = pack_weight(n((L, B)) / fl[:, None], "e2m1")
    wbp = pack_weight(n((L, N)) * 1 / np.sqrt(L) * fl[:, None], "e4m3")
    return {
        "xf": (n((K, T))).astype(np.float32),
        "fk": (np.random.uniform(0.5, 2.0, (K, 1)) / fk[:, None]).astype(np.float32),
        "w_words": wp[0],
        "w_scales": wp[1],
        "bx_words": bxp[0],
        "bx_scales": bxp[1],
        "wb_words": wbp[0],
        "wb_scales": wbp[1],
        "offs": striped8(idx),
    }


def reference(xf, fk, w_words, w_scales, bx_words, bx_scales, wb_words, wb_scales, offs):
    idx = unstriped8(offs)
    wu = unpack_weight(w_words, w_scales, "e4m3")
    bxu = unpack_weight(bx_words, bx_scales, "e2m1")
    wbu = unpack_weight(wb_words, wb_scales, "e4m3")
    u = pick8(f64(xf), idx, 64).reshape(K, B, J // B).max(axis=2) * f64(fk)
    uq = mxq(u, 0, "e4m3")
    y = wu.T @ uq + wbu.T @ bxu
    words, scales = planes(y)
    return y, words, scales

@@ -1,0 +1,163 @@
+from contextlib import ExitStack
+
+import concourse.mybir as mybir
+
+K, T, J, B, L, N = 512, 2048, 1024, 128, 512, 512
+FLOPS = 2 * (K + L) * N * B
+
+F32 = mybir.dt.float32
+BF16 = mybir.dt.bfloat16
+I32 = mybir.dt.int32
+U16 = mybir.dt.uint16
+U8 = mybir.dt.uint8
+FP8X4 = mybir.dt.float8_e4m3fn_x4
+FP4X4 = mybir.dt.float4_e2m1fn_x4
+ALU = mybir.AluOpType
+COPY = mybir.ActivationFunctionType.Copy
+
+P = 128
+PACK = 4
+BUNDLE = J // B
+W_ROW = 4
+
+
+def tile_moe_expert_heads_bundled_pl_kernel(
+    tc, xf, fk, w_words, w_scales, bx_words, bx_scales, wb_words, wb_scales, offs, out_0, out_1, out_2
+):
+    nc = tc.nc
+    with ExitStack() as ctx:
+        keep = ctx.enter_context(tc.tile_pool(name="keep", bufs=1))
+        psum = ctx.enter_context(tc.psum_pool(name="psum", bufs=1))
+
+        offsets = keep.tile([P, J // 16], U16, name="offsets")
+        x = [keep.tile([P, T], F32, name="x%d" % t, tag="x%d" % t) for t in range(PACK)]
+        picked = [keep.tile([P, J], F32, name="picked%d" % t) for t in range(PACK)]
+        top = {}
+        factor = keep.tile([P, PACK], F32, name="factor")
+        w_raw = keep.tile([P, N], I32, name="w_raw", align_bytes=64)
+        wb_raw = keep.tile([P, N], I32, name="wb_raw", align_bytes=64)
+        w_dealt = keep.tile([P, N], I32, name="w_dealt", align_bytes=64)
+        wb_dealt = keep.tile([P, N], I32, name="wb_dealt", align_bytes=64)
+        s_raw = keep.tile([P, N], U8, name="s_raw", align_bytes=64)
+        s_dealt = keep.tile([P, N], U8, name="s_dealt", align_bytes=64)
+        bx_codes = keep.tile([P, 2 * B], U8, name="bx_codes", align_bytes=64)
+        bx_plane = keep.tile([P, B], U8, name="bx_plane", align_bytes=64)
+        u_bf = keep.tile([P, B, PACK], BF16, name="u_bf", align_bytes=64)
+        u_codes = keep.tile([P, B], I32, name="u_codes", align_bytes=64)
+        u_plane = keep.tile([P, B], U8, name="u_plane", align_bytes=64)
+        y = keep.tile([P, PACK, B], F32, name="y", align_bytes=64)
+        y_bf = keep.tile([P, B, PACK], BF16, name="y_bf", align_bytes=64)
+        y_codes = keep.tile([P, B], I32, name="y_codes", align_bytes=64)
+        y_plane = keep.tile([P, B], U8, name="y_plane", align_bytes=64)
+        acc = [psum.tile([P, B], F32, name="acc%d" % t) for t in range(PACK)]
+
+        xf_rows = xf.rearrange("(p t) c -> p t c", t=PACK)
+
+        def load_scale_rows(queue, plane, first, scales):
+            rows = scales[0].bitcast(I32).rearrange("(q r) c -> r q c", r=4)
+            for r in range(4):
+                queue.dma_start(out=plane[:].bitcast(I32)[first + r : P : 32, :], in_=rows[r])
+
+        def deal(dst, src):
+            nc.vector.tensor_copy(
+                out=dst[:].rearrange("p (t m) -> p m t", t=PACK),
+                in_=src[:].rearrange("p (m t) -> p m t", t=PACK),
+            )
+
+        def gather(t):
+            nc.vector.tensor_copy(out=picked[t][:], in_=x[t][:].indirect(offsets[:]))
+
+        def largest(t):
+            top[t] = keep.tile([P, B], F32, name="top%d" % t, tag="x%d" % (t + 1))
+            nc.vector.tensor_reduce(
+                out=top[t][:],
+                in_=picked[t][:].rearrange("p (b j) -> p b j", j=BUNDLE),
+                axis=mybir.AxisListType.X,
+                op=ALU.max,
+            )
+
+        def scale_on_scalar(t):
+            nc.scalar.activation(out=u_bf[:, :, t], in_=top[t][:], func=COPY, scale=factor[:, t : t + 1])
+
+        def scale_on_vector(t):
+            nc.vector.tensor_scalar(
+                out=u_bf[:, :, t], in0=top[t][:], scalar1=factor[:, t : t + 1], scalar2=None, op0=ALU.mult
+            )
+
+        nc.gpsimd.memset(s_raw[:].bitcast(I32), 0)
+        nc.gpsimd.memset(bx_plane[:].bitcast(I32), 0)
+
+        nc.sync.dma_start(out=x[0][:], in_=xf_rows[:, 0, :])
+        nc.sync.dma_start(offsets[:], offs)
+        nc.sync.dma_start(out=x[1][:], in_=xf_rows[:, 1, :])
+        load_scale_rows(nc.sync, s_raw, W_ROW, w_scales)
+        load_scale_rows(nc.sync, s_raw, 0, wb_scales)
+        nc.sync.dma_start(out=factor[:], in_=fk.rearrange("(p t) o -> p (t o)", t=PACK))
+        nc.sync.dma_start(out=w_raw[:], in_=w_words[0].rearrange("p n r -> p (n r)").bitcast(I32))
+        nc.sync.dma_start(out=x[2][:], in_=xf_rows[:, 2, :])
+        nc.sync.dma_start(out=wb_raw[:], in_=wb_words[0].rearrange("p n r -> p (n r)").bitcast(I32))
+        nc.sync.dma_start(out=x[3][:], in_=xf_rows[:, 3, :])
+        nc.sync.dma_start(out=bx_codes[:].bitcast(I32), in_=bx_words[0].bitcast(I32))
+        load_scale_rows(nc.sync, bx_plane, 0, bx_scales)
+
+        gather(0)
+        gather(1)
+        largest(0)
+        scale_on_scalar(0)
+        deal(s_dealt, s_raw)
+        deal(w_dealt, w_raw)
+        gather(2)
+        largest(1)
+        scale_on_scalar(1)
+        deal(wb_dealt, wb_raw)
+        for t in range(PACK):
+            cols = slice(t * P, (t + 1) * P)
+            nc.tensor.matmul_mx(
+                out=acc[t][:],
+                lhsT=wb_dealt[:, cols].bitcast(FP8X4),
+                lhsT_scale=s_dealt[:, cols],
+                rhs=bx_codes[:].bitcast(FP4X4),
+                rhs_scale=bx_plane[:],
+                start=True,
+                stop=False,
+            )
+        gather(3)
+        largest(2)
+        largest(3)
+        scale_on_vector(2)
+        scale_on_vector(3)
+
+        nc.vector.quantize_mx(
+            out=u_codes[:].bitcast(FP8X4), scales=u_plane[:], in_=u_bf[:].rearrange("p b t -> p (b t)")
+        )
+        for t in range(PACK):
+            cols = slice(t * P, (t + 1) * P)
+            nc.tensor.matmul_mx(
+                out=acc[t][:],
+                lhsT=w_dealt[:, cols].bitcast(FP8X4),
+                lhsT_scale=s_dealt[W_ROW:P, cols],
+                rhs=u_codes[:].bitcast(FP8X4),
+                rhs_scale=u_plane[:],
+                start=False,
+                stop=True,
+            )
+            if t % 2 == 0:
+                nc.scalar.copy(out=y[:, t, :], in_=acc[t][:])
+            else:
+                nc.vector.tensor_copy(out=y[:, t, :], in_=acc[t][:])
+
+        nc.sync.dma_start(out=out_0.rearrange("(p t) b -> p t b", t=PACK), in_=y[:])
+        nc.vector.tensor_copy(
+            out=y_bf[:].rearrange("p (c i) t -> p c t i", i=4),
+            in_=y[:].rearrange("p t (c i) -> p c t i", i=4),
+        )
+        nc.vector.quantize_mx(
+            out=y_codes[:].bitcast(FP8X4), scales=y_plane[:], in_=y_bf[:].rearrange("p b t -> p (b t)")
+        )
+        nc.sync.dma_start(out=out_1[0].rearrange("p b r -> p (b r)").bitcast(I32), in_=y_codes[:])
+        scale_rows = out_2[0].bitcast(I32)
+        for q in range(4):
+            queue = nc.scalar if q < 2 else nc.sync
+            queue.dma_start(
+                out=scale_rows[4 * q : 4 * q + 4, :], in_=y_plane[:].bitcast(I32)[32 * q : 32 * q + 4, :]
+            )

@@ -30,9 +30,9 @@ def tile_moe_expert_heads_bundled_pl_kernel(
         psum = ctx.enter_context(tc.psum_pool(name="psum", bufs=1))
 
         offsets = keep.tile([P, J // 16], U16, name="offsets")
-        x = [keep.tile([P, T], F32, name="x%d" % t, tag="x%d" % t) for t in range(PACK)]
+        x = [keep.tile([P, T], F32, name="x%d" % t) for t in range(PACK)]
         picked = [keep.tile([P, J], F32, name="picked%d" % t) for t in range(PACK)]
-        top = {}
+        top = [keep.tile([P, B], F32, name="top%d" % t) for t in range(PACK)]
         factor = keep.tile([P, PACK], F32, name="factor")
         w_raw = keep.tile([P, N], I32, name="w_raw", align_bytes=64)
         wb_raw = keep.tile([P, N], I32, name="wb_raw", align_bytes=64)
@@ -59,22 +59,27 @@ def tile_moe_expert_heads_bundled_pl_kernel(
                 queue.dma_start(out=plane[:].bitcast(I32)[first + r : P : 32, :], in_=rows[r])
 
         def deal(dst, src):
-            nc.vector.tensor_copy(
-                out=dst[:].rearrange("p (t m) -> p m t", t=PACK),
-                in_=src[:].rearrange("p (m t) -> p m t", t=PACK),
-            )
+            for t in range(0, PACK, 2):
+                nc.gpsimd.tensor_copy(
+                    out=dst[:].rearrange("p (t m) -> p t m", t=PACK)[:, t : t + 2, :],
+                    in_=src[:].rearrange("p (m t) -> p t m", t=PACK)[:, t : t + 2, :],
+                )
 
         def gather(t):
-            nc.vector.tensor_copy(out=picked[t][:], in_=x[t][:].indirect(offsets[:]))
+            for h in range(2):
+                nc.vector.tensor_copy(
+                    out=picked[t][:, h * J // 2 : (h + 1) * J // 2],
+                    in_=x[t][:].indirect(offsets[:, h * J // 32 : (h + 1) * J // 32]),
+                )
 
         def largest(t):
-            top[t] = keep.tile([P, B], F32, name="top%d" % t, tag="x%d" % (t + 1))
-            nc.vector.tensor_reduce(
-                out=top[t][:],
-                in_=picked[t][:].rearrange("p (b j) -> p b j", j=BUNDLE),
-                axis=mybir.AxisListType.X,
-                op=ALU.max,
-            )
+            for h in range(2):
+                nc.vector.tensor_reduce(
+                    out=top[t][:, h * B // 2 : (h + 1) * B // 2],
+                    in_=picked[t][:, h * J // 2 : (h + 1) * J // 2].rearrange("p (b j) -> p b j", j=BUNDLE),
+                    axis=mybir.AxisListType.X,
+                    op=ALU.max,
+                )
 
         def scale_on_scalar(t):
             nc.scalar.activation(out=u_bf[:, :, t], in_=top[t][:], func=COPY, scale=factor[:, t : t + 1])
@@ -89,27 +94,27 @@ def tile_moe_expert_heads_bundled_pl_kernel(
 
         nc.sync.dma_start(out=x[0][:], in_=xf_rows[:, 0, :])
         nc.sync.dma_start(offsets[:], offs)
-        nc.sync.dma_start(out=x[1][:], in_=xf_rows[:, 1, :])
-        load_scale_rows(nc.sync, s_raw, W_ROW, w_scales)
-        load_scale_rows(nc.sync, s_raw, 0, wb_scales)
-        nc.sync.dma_start(out=factor[:], in_=fk.rearrange("(p t) o -> p (t o)", t=PACK))
+        for t in range(1, PACK):
+            nc.sync.dma_start(out=x[t][:], in_=xf_rows[:, t, :])
         nc.sync.dma_start(out=w_raw[:], in_=w_words[0].rearrange("p n r -> p (n r)").bitcast(I32))
-        nc.sync.dma_start(out=x[2][:], in_=xf_rows[:, 2, :])
         nc.sync.dma_start(out=wb_raw[:], in_=wb_words[0].rearrange("p n r -> p (n r)").bitcast(I32))
-        nc.sync.dma_start(out=x[3][:], in_=xf_rows[:, 3, :])
         nc.sync.dma_start(out=bx_codes[:].bitcast(I32), in_=bx_words[0].bitcast(I32))
+        nc.sync.dma_start(out=factor[:], in_=fk.rearrange("(p t) o -> p (t o)", t=PACK))
+        load_scale_rows(nc.sync, s_raw, 0, wb_scales)
+        load_scale_rows(nc.sync, s_raw, W_ROW, w_scales)
         load_scale_rows(nc.sync, bx_plane, 0, bx_scales)
 
         gather(0)
-        gather(1)
         largest(0)
         scale_on_scalar(0)
-        deal(s_dealt, s_raw)
-        deal(w_dealt, w_raw)
-        gather(2)
+        gather(1)
         largest(1)
         scale_on_scalar(1)
+        gather(2)
+        largest(2)
+        deal(w_dealt, w_raw)
         deal(wb_dealt, wb_raw)
+        deal(s_dealt, s_raw)
         for t in range(PACK):
             cols = slice(t * P, (t + 1) * P)
             nc.tensor.matmul_mx(
@@ -122,7 +127,6 @@ def tile_moe_expert_heads_bundled_pl_kernel(
                 stop=False,
             )
         gather(3)
-        largest(2)
         largest(3)
         scale_on_vector(2)
         scale_on_vector(3)
@@ -147,13 +151,18 @@ def tile_moe_expert_heads_bundled_pl_kernel(
                 nc.vector.tensor_copy(out=y[:, t, :], in_=acc[t][:])
 
         nc.sync.dma_start(out=out_0.rearrange("(p t) b -> p t b", t=PACK), in_=y[:])
-        nc.vector.tensor_copy(
-            out=y_bf[:].rearrange("p (c i) t -> p c t i", i=4),
-            in_=y[:].rearrange("p t (c i) -> p c t i", i=4),
-        )
-        nc.vector.quantize_mx(
-            out=y_codes[:].bitcast(FP8X4), scales=y_plane[:], in_=y_bf[:].rearrange("p b t -> p (b t)")
-        )
+        halves = [slice(0, B // 2), slice(B // 2, B)]
+        for half in halves:
+            nc.vector.tensor_copy(
+                out=y_bf[:, half, :].rearrange("p (c i) t -> p c t i", i=4),
+                in_=y[:, :, half].rearrange("p t (c i) -> p c t i", i=4),
+            )
+        for half in halves:
+            nc.vector.quantize_mx(
+                out=y_codes[:, half].bitcast(FP8X4),
+                scales=y_plane[:, half],
+                in_=y_bf[:, half, :].rearrange("p b t -> p (b t)"),
+            )
         nc.sync.dma_start(out=out_1[0].rearrange("p b r -> p (b r)").bitcast(I32), in_=y_codes[:])
         scale_rows = out_2[0].bitcast(I32)
         for q in range(4):

@@ -30,16 +30,13 @@ def tile_moe_expert_heads_bundled_pl_kernel(
         psum = ctx.enter_context(tc.psum_pool(name="psum", bufs=1))
 
         offsets = keep.tile([P, J // 16], U16, name="offsets")
-        x = [keep.tile([P, T], F32, name="x%d" % t) for t in range(PACK)]
+        x = [keep.tile([P, T], F32, name="x%d" % t, tag="x%d" % t, align_bytes=64) for t in range(PACK)]
         picked = [keep.tile([P, J], F32, name="picked%d" % t) for t in range(PACK)]
         top = [keep.tile([P, B], F32, name="top%d" % t) for t in range(PACK)]
         factor = keep.tile([P, PACK], F32, name="factor")
         w_raw = keep.tile([P, N], I32, name="w_raw", align_bytes=64)
         wb_raw = keep.tile([P, N], I32, name="wb_raw", align_bytes=64)
-        w_dealt = keep.tile([P, N], I32, name="w_dealt", align_bytes=64)
-        wb_dealt = keep.tile([P, N], I32, name="wb_dealt", align_bytes=64)
         s_raw = keep.tile([P, N], U8, name="s_raw", align_bytes=64)
-        s_dealt = keep.tile([P, N], U8, name="s_dealt", align_bytes=64)
         bx_codes = keep.tile([P, 2 * B], U8, name="bx_codes", align_bytes=64)
         bx_plane = keep.tile([P, B], U8, name="bx_plane", align_bytes=64)
         u_bf = keep.tile([P, B, PACK], BF16, name="u_bf", align_bytes=64)
@@ -58,12 +55,14 @@ def tile_moe_expert_heads_bundled_pl_kernel(
             for r in range(4):
                 queue.dma_start(out=plane[:].bitcast(I32)[first + r : P : 32, :], in_=rows[r])
 
-        def deal(dst, src):
+        def deal(src, dtype, after):
+            dst = keep.tile([P, N], dtype, name="dealt%d" % after, tag="x%d" % after, align_bytes=64)
             for t in range(0, PACK, 2):
                 nc.gpsimd.tensor_copy(
                     out=dst[:].rearrange("p (t m) -> p t m", t=PACK)[:, t : t + 2, :],
                     in_=src[:].rearrange("p (m t) -> p t m", t=PACK)[:, t : t + 2, :],
                 )
+            return dst
 
         def gather(t):
             for h in range(2):
@@ -84,9 +83,9 @@ def tile_moe_expert_heads_bundled_pl_kernel(
         def scale_on_scalar(t):
             nc.scalar.activation(out=u_bf[:, :, t], in_=top[t][:], func=COPY, scale=factor[:, t : t + 1])
 
-        def scale_on_vector(t):
+        def scale_on_vector(t, cols):
             nc.vector.tensor_scalar(
-                out=u_bf[:, :, t], in0=top[t][:], scalar1=factor[:, t : t + 1], scalar2=None, op0=ALU.mult
+                out=u_bf[:, cols, t], in0=top[t][:, cols], scalar1=factor[:, t : t + 1], scalar2=None, op0=ALU.mult
             )
 
         nc.gpsimd.memset(s_raw[:].bitcast(I32), 0)
@@ -94,27 +93,28 @@ def tile_moe_expert_heads_bundled_pl_kernel(
 
         nc.sync.dma_start(out=x[0][:], in_=xf_rows[:, 0, :])
         nc.sync.dma_start(offsets[:], offs)
-        for t in range(1, PACK):
-            nc.sync.dma_start(out=x[t][:], in_=xf_rows[:, t, :])
         nc.sync.dma_start(out=w_raw[:], in_=w_words[0].rearrange("p n r -> p (n r)").bitcast(I32))
+        nc.sync.dma_start(out=x[1][:], in_=xf_rows[:, 1, :])
         nc.sync.dma_start(out=wb_raw[:], in_=wb_words[0].rearrange("p n r -> p (n r)").bitcast(I32))
-        nc.sync.dma_start(out=bx_codes[:].bitcast(I32), in_=bx_words[0].bitcast(I32))
-        nc.sync.dma_start(out=factor[:], in_=fk.rearrange("(p t) o -> p (t o)", t=PACK))
+        nc.sync.dma_start(out=x[2][:], in_=xf_rows[:, 2, :])
         load_scale_rows(nc.sync, s_raw, 0, wb_scales)
         load_scale_rows(nc.sync, s_raw, W_ROW, w_scales)
+        nc.sync.dma_start(out=x[3][:], in_=xf_rows[:, 3, :])
+        nc.sync.dma_start(out=bx_codes[:].bitcast(I32), in_=bx_words[0].bitcast(I32))
+        nc.sync.dma_start(out=factor[:], in_=fk.rearrange("(p t) o -> p (t o)", t=PACK))
         load_scale_rows(nc.sync, bx_plane, 0, bx_scales)
 
         gather(0)
+        w_dealt = deal(w_raw, I32, 0)
         largest(0)
         scale_on_scalar(0)
         gather(1)
+        wb_dealt = deal(wb_raw, I32, 1)
         largest(1)
         scale_on_scalar(1)
         gather(2)
+        s_dealt = deal(s_raw, U8, 2)
         largest(2)
-        deal(w_dealt, w_raw)
-        deal(wb_dealt, wb_raw)
-        deal(s_dealt, s_raw)
         for t in range(PACK):
             cols = slice(t * P, (t + 1) * P)
             nc.tensor.matmul_mx(
@@ -128,12 +128,16 @@ def tile_moe_expert_heads_bundled_pl_kernel(
             )
         gather(3)
         largest(3)
-        scale_on_vector(2)
-        scale_on_vector(3)
-
-        nc.vector.quantize_mx(
-            out=u_codes[:].bitcast(FP8X4), scales=u_plane[:], in_=u_bf[:].rearrange("p b t -> p (b t)")
-        )
+        halves = [slice(0, B // 2), slice(B // 2, B)]
+        scale_on_vector(3, halves[0])
+        scale_on_vector(2, slice(0, B))
+        scale_on_vector(3, halves[1])
+        for half in halves:
+            nc.vector.quantize_mx(
+                out=u_codes[:, half].bitcast(FP8X4),
+                scales=u_plane[:, half],
+                in_=u_bf[:, half, :].rearrange("p b t -> p (b t)"),
+            )
         for t in range(PACK):
             cols = slice(t * P, (t + 1) * P)
             nc.tensor.matmul_mx(
@@ -145,13 +149,12 @@ def tile_moe_expert_heads_bundled_pl_kernel(
                 start=False,
                 stop=True,
             )
-            if t % 2 == 0:
+            if t < 2:
                 nc.scalar.copy(out=y[:, t, :], in_=acc[t][:])
             else:
                 nc.vector.tensor_copy(out=y[:, t, :], in_=acc[t][:])
 
         nc.sync.dma_start(out=out_0.rearrange("(p t) b -> p t b", t=PACK), in_=y[:])
-        halves = [slice(0, B // 2), slice(B // 2, B)]
         for half in halves:
             nc.vector.tensor_copy(
                 out=y_bf[:, half, :].rearrange("p (c i) t -> p c t i", i=4),

from contextlib import ExitStack

import concourse.mybir as mybir

K, T, J, B, L, N = 512, 2048, 1024, 128, 512, 512
FLOPS = 2 * (K + L) * N * B

F32 = mybir.dt.float32
BF16 = mybir.dt.bfloat16
I32 = mybir.dt.int32
U16 = mybir.dt.uint16
U8 = mybir.dt.uint8
FP8X4 = mybir.dt.float8_e4m3fn_x4
FP4X4 = mybir.dt.float4_e2m1fn_x4
ALU = mybir.AluOpType
COPY = mybir.ActivationFunctionType.Copy

P = 128
PACK = 4
BUNDLE = J // B
W_ROW = 4


def tile_moe_expert_heads_bundled_pl_kernel(
    tc, xf, fk, w_words, w_scales, bx_words, bx_scales, wb_words, wb_scales, offs, out_0, out_1, out_2
):
    nc = tc.nc
    with ExitStack() as ctx:
        keep = ctx.enter_context(tc.tile_pool(name="keep", bufs=1))
        psum = ctx.enter_context(tc.psum_pool(name="psum", bufs=1))

        offsets = keep.tile([P, J // 16], U16, name="offsets")
        x = [keep.tile([P, T], F32, name="x%d" % t, tag="x%d" % t, align_bytes=64) for t in range(PACK)]
        picked = [keep.tile([P, J], F32, name="picked%d" % t) for t in range(PACK)]
        top = [keep.tile([P, B], F32, name="top%d" % t) for t in range(PACK)]
        factor = keep.tile([P, PACK], F32, name="factor")
        w_raw = keep.tile([P, N], I32, name="w_raw", align_bytes=64)
        wb_raw = keep.tile([P, N], I32, name="wb_raw", align_bytes=64)
        s_raw = keep.tile([P, N], U8, name="s_raw", align_bytes=64)
        bx_codes = keep.tile([P, 2 * B], U8, name="bx_codes", align_bytes=64)
        bx_plane = keep.tile([P, B], U8, name="bx_plane", align_bytes=64)
        u_bf = keep.tile([P, B, PACK], BF16, name="u_bf", align_bytes=64)
        u_codes = keep.tile([P, B], I32, name="u_codes", align_bytes=64)
        u_plane = keep.tile([P, B], U8, name="u_plane", align_bytes=64)
        y = keep.tile([P, PACK, B], F32, name="y", align_bytes=64)
        y_bf = keep.tile([P, B, PACK], BF16, name="y_bf", align_bytes=64)
        y_codes = keep.tile([P, B], I32, name="y_codes", align_bytes=64)
        y_plane = keep.tile([P, B], U8, name="y_plane", align_bytes=64)
        acc = [psum.tile([P, B], F32, name="acc%d" % t) for t in range(PACK)]

        xf_rows = xf.rearrange("(p t) c -> p t c", t=PACK)

        def load_scale_rows(queue, plane, first, scales):
            rows = scales[0].bitcast(I32).rearrange("(q r) c -> r q c", r=4)
            for r in range(4):
                queue.dma_start(out=plane[:].bitcast(I32)[first + r : P : 32, :], in_=rows[r])

        def deal(src, dtype, after):
            dst = keep.tile([P, N], dtype, name="dealt%d" % after, tag="x%d" % after, align_bytes=64)
            for t in range(0, PACK, 2):
                nc.gpsimd.tensor_copy(
                    out=dst[:].rearrange("p (t m) -> p t m", t=PACK)[:, t : t + 2, :],
                    in_=src[:].rearrange("p (m t) -> p t m", t=PACK)[:, t : t + 2, :],
                )
            return dst

        def gather(t):
            for h in range(2):
                nc.vector.tensor_copy(
                    out=picked[t][:, h * J // 2 : (h + 1) * J // 2],
                    in_=x[t][:].indirect(offsets[:, h * J // 32 : (h + 1) * J // 32]),
                )

        def largest(t):
            for h in range(2):
                nc.vector.tensor_reduce(
                    out=top[t][:, h * B // 2 : (h + 1) * B // 2],
                    in_=picked[t][:, h * J // 2 : (h + 1) * J // 2].rearrange("p (b j) -> p b j", j=BUNDLE),
                    axis=mybir.AxisListType.X,
                    op=ALU.max,
                )

        def scale_on_scalar(t):
            nc.scalar.activation(out=u_bf[:, :, t], in_=top[t][:], func=COPY, scale=factor[:, t : t + 1])

        def scale_on_vector(t, cols):
            nc.vector.tensor_scalar(
                out=u_bf[:, cols, t], in0=top[t][:, cols], scalar1=factor[:, t : t + 1], scalar2=None, op0=ALU.mult
            )

        nc.gpsimd.memset(s_raw[:].bitcast(I32), 0)
        nc.gpsimd.memset(bx_plane[:].bitcast(I32), 0)

        nc.sync.dma_start(out=x[0][:], in_=xf_rows[:, 0, :])
        nc.sync.dma_start(offsets[:], offs)
        nc.sync.dma_start(out=w_raw[:], in_=w_words[0].rearrange("p n r -> p (n r)").bitcast(I32))
        nc.sync.dma_start(out=x[1][:], in_=xf_rows[:, 1, :])
        nc.sync.dma_start(out=wb_raw[:], in_=wb_words[0].rearrange("p n r -> p (n r)").bitcast(I32))
        nc.sync.dma_start(out=x[2][:], in_=xf_rows[:, 2, :])
        load_scale_rows(nc.sync, s_raw, 0, wb_scales)
        load_scale_rows(nc.sync, s_raw, W_ROW, w_scales)
        nc.sync.dma_start(out=x[3][:], in_=xf_rows[:, 3, :])
        nc.sync.dma_start(out=bx_codes[:].bitcast(I32), in_=bx_words[0].bitcast(I32))
        nc.sync.dma_start(out=factor[:], in_=fk.rearrange("(p t) o -> p (t o)", t=PACK))
        load_scale_rows(nc.sync, bx_plane, 0, bx_scales)

        gather(0)
        w_dealt = deal(w_raw, I32, 0)
        largest(0)
        scale_on_scalar(0)
        gather(1)
        wb_dealt = deal(wb_raw, I32, 1)
        largest(1)
        scale_on_scalar(1)
        gather(2)
        s_dealt = deal(s_raw, U8, 2)
        largest(2)
        for t in range(PACK):
            cols = slice(t * P, (t + 1) * P)
            nc.tensor.matmul_mx(
                out=acc[t][:],
                lhsT=wb_dealt[:, cols].bitcast(FP8X4),
                lhsT_scale=s_dealt[:, cols],
                rhs=bx_codes[:].bitcast(FP4X4),
                rhs_scale=bx_plane[:],
                start=True,
                stop=False,
            )
        gather(3)
        largest(3)
        halves = [slice(0, B // 2), slice(B // 2, B)]
        scale_on_vector(3, halves[0])
        scale_on_vector(2, slice(0, B))
        scale_on_vector(3, halves[1])
        for half in halves:
            nc.vector.quantize_mx(
                out=u_codes[:, half].bitcast(FP8X4),
                scales=u_plane[:, half],
                in_=u_bf[:, half, :].rearrange("p b t -> p (b t)"),
            )
        for t in range(PACK):
            cols = slice(t * P, (t + 1) * P)
            nc.tensor.matmul_mx(
                out=acc[t][:],
                lhsT=w_dealt[:, cols].bitcast(FP8X4),
                lhsT_scale=s_dealt[W_ROW:P, cols],
                rhs=u_codes[:].bitcast(FP8X4),
                rhs_scale=u_plane[:],
                start=False,
                stop=True,
            )
            if t < 2:
                nc.scalar.copy(out=y[:, t, :], in_=acc[t][:])
            else:
                nc.vector.tensor_copy(out=y[:, t, :], in_=acc[t][:])

        nc.sync.dma_start(out=out_0.rearrange("(p t) b -> p t b", t=PACK), in_=y[:])
        for half in halves:
            nc.vector.tensor_copy(
                out=y_bf[:, half, :].rearrange("p (c i) t -> p c t i", i=4),
                in_=y[:, :, half].rearrange("p t (c i) -> p c t i", i=4),
            )
        for half in halves:
            nc.vector.quantize_mx(
                out=y_codes[:, half].bitcast(FP8X4),
                scales=y_plane[:, half],
                in_=y_bf[:, half, :].rearrange("p b t -> p (b t)"),
            )
        nc.sync.dma_start(out=out_1[0].rearrange("p b r -> p (b r)").bitcast(I32), in_=y_codes[:])
        scale_rows = out_2[0].bitcast(I32)
        for q in range(4):
            queue = nc.scalar if q < 2 else nc.sync
            queue.dma_start(
                out=scale_rows[4 * q : 4 * q + 4, :], in_=y_plane[:].bitcast(I32)[32 * q : 32 * q + 4, :]
            )
